import numpy as np
import ml_dtypes


def mxq(x, axis, fmt="e4m3"):
    dtype, down = {"e4m3": (ml_dtypes.float8_e4m3fn, 7), "e5m2": (ml_dtypes.float8_e5m2, 14)}[fmt]
    v = np.moveaxis(np.asarray(x, np.float32).astype(ml_dtypes.bfloat16).astype(np.float64), axis, -1)
    blocks = v.reshape(v.shape[:-1] + (-1, 32))
    amax = np.abs(blocks).max(-1, keepdims=True)
    byte = np.maximum(np.where(amax > 0, np.frexp(amax)[1] - 1 + 127, 0) - down, 1)
    scale = np.exp2(byte - 127.0)
    codes = (blocks / scale).astype(np.float32).astype(dtype).astype(np.float64)
    return np.moveaxis((codes * scale).reshape(v.shape), -1, axis)


WIDE = False


def mx_kscale(k):
    if not WIDE:
        return np.ones(k)
    levels = np.array([30, -30])
    if k % 512:
        return np.exp2(np.random.permutation(np.resize(levels, k // 32))).repeat(32)
    a = np.empty((k // 512, 16))
    for p in range(k // 512):
        a[p, :8] = np.random.permutation(np.resize(levels, 8))
        for g in range(8):
            far = levels[np.abs(levels - a[p, g]) >= 10]
            a[p, g + 8] = far[np.random.randint(len(far))]
    return np.exp2(a.ravel()).repeat(32)


BF16 = ml_dtypes.bfloat16


def bf(x):
    return np.asarray(x, np.float32).astype(BF16)


def f64(x):
    return np.asarray(x).astype(np.float64)


P, C = 1536, 1024


def setup_inputs():
    u, t = mx_kscale(P), mx_kscale(C)
    x = np.random.standard_normal((P, C)) * np.abs(np.random.standard_normal((P, C)))
    a = np.random.standard_normal((P, P)) / np.sqrt(2 * P)
    w = np.random.standard_normal((C, C)) / np.sqrt(2 * C)
    cell = 1 + 0.1 * np.random.standard_normal(P)
    chan = 1 + 0.1 * np.random.standard_normal(C)
    return {"x": bf(x * u[:, None] * t),
            "a": bf(a / u * u[:, None]),
            "w": bf(w / t[:, None] * t),
            "cell": bf(cell / u),
            "chan": bf(chan / t),
            "b": bf(0.3 * np.random.standard_normal(C))}


def reference(x, a, w, cell, chan, b):
    x, a, w, cell, chan, b = f64(x), f64(a), f64(w), f64(cell), f64(chan), f64(b)
    xg = mxq(x, 0, "e4m3")
    xc = mxq(x, 1, "e5m2")
    grid = mxq(a, 1, "e4m3") @ xg
    mix = xc @ mxq(w, 0, "e4m3")
    z = grid + mix
    z = z * cell[:, None] * chan
    return np.tanh(z + b)

@@ -1,0 +1,244 @@
+from contextlib import ExitStack
+
+import concourse.mybir as mybir
+from concourse.masks import make_identity
+
+CELLS, CHANNELS = 1536, 1024
+FLOPS = 2 * CELLS * CELLS * CHANNELS + 2 * CELLS * CHANNELS * CHANNELS
+
+F32 = mybir.dt.float32
+BF16 = mybir.dt.bfloat16
+U32 = mybir.dt.uint32
+U8 = mybir.dt.uint8
+E4M3 = mybir.dt.float8_e4m3fn_x4
+E5M2 = mybir.dt.float8_e5m2_x4
+ALU = mybir.AluOpType
+ACT = mybir.ActivationFunctionType
+
+P = 128
+J = 4
+HALF = 512
+GROUPS = CELLS // 512
+PASSES = {"x": CHANNELS // 512, "a": CELLS // 512}
+LAID = {"w": CHANNELS // 512, "x": CELLS // 512}
+
+
+def producers(op):
+    kind, key = op[0], op[1:]
+    if kind == "copy":
+        return [("turn",) + key]
+    if kind == "quant":
+        return [("copy",) + key + (jp,) for jp in range(2)]
+    if kind == "quantl":
+        return [("lay",) + key]
+    if kind == "mix":
+        g, j, h = key
+        return [("quant", "x", g, s) for s in range(PASSES["x"])] + [("quantl", "w", s, h) for s in range(LAID["w"])]
+    if kind == "grid":
+        g, j, h = key
+        return [("mix",) + key] + [("quant", "a", g, s) for s in range(PASSES["a"])] + [("quantl", "x", s, h) for s in range(LAID["x"])]
+    before = {"scale": "grid", "bias": "scale", "tanh": "bias", "colcopy": "cols", "spread": "colcopy", "spreadcopy": "spread"}
+    if kind in ("spread",):
+        return [("colcopy",)]
+    return [(before[kind],) + key] if kind in before else []
+
+
+def tile_weather_grid_channel_mixing_s2_kernel(tc, x, a, w, cell, chan, b, out):
+    nc = tc.nc
+    with ExitStack() as ctx:
+        keep = ctx.enter_context(tc.tile_pool(name="keep", bufs=1))
+        stage = ctx.enter_context(tc.tile_pool(name="stage", bufs=12))
+        epi = ctx.enter_context(tc.tile_pool(name="epi", bufs=4))
+        psum = ctx.enter_context(tc.psum_pool(name="psum", bufs=8))
+        ctx.enter_context(tc.manual_schedule())
+
+        def kept(shape, dtype, name):
+            return keep.tile(shape, dtype, name=name, align_bytes=64)
+
+        x_v = x.rearrange("(g p j) c -> g p j c", p=P, j=J)
+        a_v = a.rearrange("(g p j) c -> g p j c", p=P, j=J)
+        w_v = w.rearrange("(s p j) c -> s p j c", p=P, j=J)
+        out_v = out.rearrange("(g p j) c -> g p j c", p=P, j=J)
+
+        raw = {}
+        for g in range(GROUPS):
+            raw["x", g] = kept([P, J, CHANNELS], BF16, "x_raw%d" % g)
+            raw["a", g] = kept([P, J, CELLS], BF16, "a_raw%d" % g)
+        for s in range(LAID["w"]):
+            for h in range(2):
+                raw["w", s, h] = kept([P, J, HALF], BF16, "w_raw%d%d" % (s, h))
+        rows = kept([P, P], BF16, "rows")
+        cells = kept([P, GROUPS, J], BF16, "cells")
+        warm = kept([P, 1], F32, "warm")
+        ident = kept([P, P], F32, "ident")
+        ident_bf = kept([P, P], BF16, "ident_bf")
+        cols = kept([P, 16], BF16, "cols")
+        spread = [kept([P, CHANNELS], BF16, "spread%d" % v) for v in range(2)]
+
+        nc.vector.memset(warm[:], 0.0)
+        nc.scalar.activation(out=warm[:], in_=warm[:], func=ACT.Tanh)
+        nc.vector.memset(rows[:], 0.0)
+        make_identity(nc, ident[:])
+        nc.vector.tensor_copy(out=ident_bf[:], in_=ident[:])
+
+        def load(k, g):
+            view = {"x": x_v, "a": a_v}[k]
+            for jp in range(2):
+                js = slice(2 * jp, 2 * jp + 2)
+                nc.sync.dma_start(out=raw[k, g][:, js, :], in_=view[g][:, js, :])
+
+        def load_w(h):
+            for s in range(LAID["w"]):
+                nc.sync.dma_start(out=raw["w", s, h][:], in_=w_v[s][:, :, h * HALF : (h + 1) * HALF])
+
+        load("x", 0)
+        nc.sync.dma_start(out=rows[0:8, :], in_=chan.rearrange("(m n) -> m n", n=P))
+        nc.sync.dma_start(out=rows[8:16, :], in_=b.rearrange("(m n) -> m n", n=P))
+        load("x", 1)
+        load_w(0)
+        load("x", 2)
+        load("a", 0)
+        nc.sync.dma_start(out=cells[:], in_=cell.rearrange("(g p j) -> p g j", p=P, j=J))
+        load("a", 1)
+        load("a", 2)
+        load_w(1)
+
+        codes, scales = {}, {}
+        for k in "xa":
+            for g in range(GROUPS):
+                for s in range(PASSES[k]):
+                    codes[k, "t", g, s] = kept([P, HALF], U32, "c%st%d%d" % (k, g, s))
+                    scales[k, "t", g, s] = kept([P, HALF], U8, "s%st%d%d" % (k, g, s))
+        for k in "xw":
+            for s in range(LAID[k]):
+                for h in range(2):
+                    codes[k, "l", s, h] = kept([P, HALF], U32, "c%sl%d%d" % (k, s, h))
+                    scales[k, "l", s, h] = kept([P, HALF], U8, "s%sl%d%d" % (k, s, h))
+
+        tiles = {}
+
+        def bank(name, dtype=F32):
+            return psum.tile([P, 512 if dtype == F32 else 1024], dtype, name=name, tag="bank")
+
+        def copier(eng):
+            return nc.vector.tensor_copy if eng == "vector" else nc.scalar.copy
+
+        def emit(eng, op):
+            kind, key = op[0], op[1:]
+            if kind == "turn":
+                k, g, s, jp = key
+                width = {"x": CHANNELS, "a": CELLS}[k]
+                words = raw[k, g][:].rearrange("p j k -> p (j k)").bitcast(F32)
+                tiles[op] = tp = bank("tp")
+                for jj in range(2):
+                    for u in range(2):
+                        first = (2 * jp + jj) * (width // 2) + 256 * s
+                        q = 2 * jj + u
+                        nc.tensor.transpose(tp[:, q * P : (q + 1) * P], words[:, first + u : first + 256 : 2], ident[:])
+            elif kind == "copy":
+                k, g, s, jp = key
+                if ("grp", k, g, s) not in tiles:
+                    tiles["grp", k, g, s] = stage.tile([P, J * HALF], BF16, name="grp", align_bytes=64)
+                grp = tiles["grp", k, g, s]
+                o = grp[:].bitcast(F32)[:, jp * 512 : (jp + 1) * 512].rearrange("p (jj m u) -> p jj m u", jj=2, u=2)
+                i = tiles[("turn",) + key][:].rearrange("p (jj u m) -> p jj m u", jj=2, u=2)
+                copier(eng)(out=o, in_=i)
+            elif kind == "quant":
+                k, g, s = key
+                fmt = E5M2 if k == "x" else E4M3
+                nc.vector.quantize_mx(out=codes[k, "t", g, s][:].bitcast(fmt), scales=scales[k, "t", g, s][:], in_=tiles["grp", k, g, s][:])
+            elif kind == "lay":
+                k, s, h = key
+                tiles[op] = grp = stage.tile([P, J * HALF], BF16, name="grp", align_bytes=64)
+                src = raw["w", s, h][:] if k == "w" else raw["x", s][:, :, h * HALF : (h + 1) * HALF]
+                copier(eng)(out=grp[:].rearrange("p (c i j) -> p c j i", i=4, j=J), in_=src.rearrange("p j (c i) -> p c j i", i=4))
+            elif kind == "quantl":
+                k, s, h = key
+                nc.vector.quantize_mx(out=codes[k, "l", s, h][:].bitcast(E4M3), scales=scales[k, "l", s, h][:], in_=tiles["lay", k, s, h][:])
+            elif kind in ("mix", "grid"):
+                g, j, h = key
+                if kind == "mix":
+                    tiles[("acc",) + key] = bank("acc")
+                k, r, fmt = ("x", "w", E5M2) if kind == "mix" else ("a", "x", E4M3)
+                js = slice(j * P, (j + 1) * P)
+                for s in range(PASSES[k]):
+                    nc.tensor.matmul_mx(
+                        out=tiles[("acc",) + key][:],
+                        lhsT=codes[k, "t", g, s][:, js].bitcast(fmt),
+                        lhsT_scale=scales[k, "t", g, s][:, js],
+                        rhs=codes[r, "l", s, h][:].bitcast(E4M3),
+                        rhs_scale=scales[r, "l", s, h][:],
+                        start=(kind == "mix" and s == 0),
+                        stop=(kind == "grid" and s == PASSES[k] - 1),
+                    )
+            elif kind == "scale":
+                g, j, h = key
+                tiles[op] = z = epi.tile([P, HALF], F32, name="z")
+                nc.vector.scalar_tensor_tensor(
+                    out=z[:], in0=tiles[("acc",) + key][:], scalar=cells[:, g, j : j + 1], in1=spread[0][:, h * HALF : (h + 1) * HALF], op0=ALU.mult, op1=ALU.mult
+                )
+            elif kind == "bias":
+                g, j, h = key
+                tiles[op] = y = epi.tile([P, HALF], F32, name="y")
+                nc.vector.tensor_tensor(out=y[:], in0=tiles[("scale",) + key][:], in1=spread[1][:, h * HALF : (h + 1) * HALF], op=ALU.add)
+            elif kind == "tanh":
+                g, j, h = key
+                o = epi.tile([P, HALF], F32, name="o")
+                nc.scalar.activation(out=o[:], in_=tiles[("bias",) + key][:], func=ACT.Tanh)
+                nc.sync.dma_start(out=out_v[g][:, j, h * HALF : (h + 1) * HALF], in_=o[:])
+            elif kind == "cols":
+                tiles[op] = ps = bank("cols_ps", BF16)
+                nc.tensor.transpose(ps[:, 0:P], rows[:], ident_bf[:])
+            elif kind == "colcopy":
+                nc.vector.tensor_copy(out=cols[:], in_=tiles[("cols",)][:, 0:16])
+            elif kind == "spread":
+                v = key[0]
+                tiles[op] = ps = bank("spread_ps", BF16)
+                for m in range(8):
+                    nc.tensor.transpose(ps[:, m * P : (m + 1) * P], cols[:, 8 * v + m : 8 * v + m + 1].to_broadcast([P, P]), ident_bf[:])
+            elif kind == "spreadcopy":
+                copier(eng)(out=spread[key[0]][:], in_=tiles[("spread",) + key][:])
+
+        def turns(kind, k, g):
+            return [(kind, k, g, s, jp) for jp in range(2) for s in range(PASSES[k])]
+
+        def quants(k, g):
+            return [("quant", k, g, s) for s in range(PASSES[k])]
+
+        units = [(g, j, h) for h in range(2) for g in range(GROUPS) for j in range(J)]
+        first = units[:J]
+        tensor = turns("turn", "x", 0) + [("cols",), ("spread", 0), ("spread", 1)] + turns("turn", "x", 1) + turns("turn", "x", 2) + turns("turn", "a", 0)
+        tensor += [("mix",) + u for u in first]
+        tensor += turns("turn", "a", 1)
+        tensor += [("grid",) + u for u in first]
+        tensor += turns("turn", "a", 2)
+        for u in units[J:]:
+            tensor += [("mix",) + u, ("grid",) + u]
+
+        lay = lambda k, s, h: ("lay", k, s, h)
+        ql = lambda k, s, h: ("quantl", k, s, h)
+        scalar = turns("copy", "x", 0) + [("spreadcopy", 0), ("spreadcopy", 1)] + turns("copy", "x", 1) + [lay("w", 0, 0)] + turns("copy", "x", 2)[:2] + [lay("x", 2, 0)]
+        scalar += turns("copy", "a", 0) + turns("copy", "a", 1) + [lay("x", 1, 1)] + turns("copy", "a", 2)
+        vector = [lay("x", 0, 0), ("colcopy",), lay("x", 1, 0)] + quants("x", 0) + [lay("w", 1, 0), ql("x", 0, 0)] + quants("x", 1)
+        vector += [ql("w", 0, 0), ql("w", 1, 0)] + turns("copy", "x", 2)[2:] + [ql("x", 1, 0)] + quants("x", 2) + [ql("x", 2, 0)]
+        vector += quants("a", 0) + [lay("x", 0, 1)] + quants("a", 1) + [ql("x", 0, 1)]
+        v_after = {0: [lay("x", 2, 1)], 2: quants("a", 2)[:1], 3: quants("a", 2)[1:2], 4: quants("a", 2)[2:] + [ql("x", 1, 1)],
+                   5: [lay("w", 0, 1)], 6: [ql("x", 2, 1)], 7: [ql("w", 0, 1)], 8: [ql("w", 1, 1)]}
+        s_after = {0: [lay("w", 1, 1)]}
+        for n, u in enumerate(units):
+            vector.append(("scale",) + u)
+            if n:
+                vector.append(("bias",) + units[n - 1])
+            vector += v_after.get(n, [])
+            scalar.append(("tanh",) + u)
+            scalar += s_after.get(n, [])
+        vector.append(("bias",) + units[-1])
+
+        queues = {"tensor": tensor, "vector": vector, "scalar": scalar}
+        done = set()
+        while any(queues.values()):
+            for eng, queue in queues.items():
+                if queue and all(d in done for d in producers(queue[0])):
+                    op = queue.pop(0)
+                    emit(eng, op)
+                    done.add(op)

@@ -20,11 +20,29 @@ J = 4
 HALF = 512
 GROUPS = CELLS // 512
 PASSES = {"x": CHANNELS // 512, "a": CELLS // 512}
+SORTED = [("a", 1), ("a", 2)]
+TENSOR = """
+Tx00 Tx01 X Tx11 Tx10 Tx20 Tx21 Ta00 Ta01 M000 M010 Ta10 M020 Ta11 G000 G010 G020 M030 Ta21 M100 M110 G030 G100 M120
+G110 M130 G120 Ta20 M200 M210 G130 M220 M230 G200 G210 G220 M001 G230 M011 M021 M031 M101 G001 G011 G021 G031 G101 M111
+G111 M121 G121 M131 G131 M201 G201 M211 G211 M221 G221 M231 G231
+"""
+VECTOR = """
+Ix01 Ix00 Qx01 Qx00 Lx01 Ix20 Cx10 Iw10 Qx10 Lw10 Lx00 Lw00 Lx10 Lx20 Pa10 Qa00 Pa11 Qa02 Qa01 Qx21 Qx11 Qx20 Qa10 S0.0
+Qa12 S0.1 Qa11 S1.0 A0 Pa20 S1.1 S2.0 A1 S2.1 Lw11 A2 S3.0 Qa20 Qa21 Qa22 S3.1 Lw01 Lx11 A3 S4.0 S4.1 S5.0 Lx21 S5.1 A4
+A5 S6.0 S6.1 S7.0 S7.1 A6 S8.0 A7 S8.1 S9.0 A8 S9.1 S10.0 A9 A10 S11.0 S12.0 A11 A12 S13.0 A13
+"""
+SCALAR = """
+Cx00 Cx01 cc Ix10 Z0 Cx11 Iw00 Cx20 Ca00 Ca01 Cx21 Ca10 Ca11 Pa21 Z1 Iw01 Iw11 Ca21 Ca20 Ix11 Ix21 H0 H1 H2 H3 H4 H5 H6
+H7 H8 H9 H10 H11 H12 H13
+"""
 LAID = {"w": CHANNELS // 512, "x": CELLS // 512}
 
 
 def producers(op):
     kind, key = op[0], op[1:]
+    if kind == "turn":
+        k, g, s, jp = key
+        return [("sort",) + key] if (k, g) in SORTED else []
     if kind == "copy":
         return [("turn",) + key]
     if kind == "quant":
@@ -34,10 +52,15 @@ def producers(op):
     if kind == "mix":
         g, j, h = key
         return [("quant", "x", g, s) for s in range(PASSES["x"])] + [("quantl", "w", s, h) for s in range(LAID["w"])]
+    if kind == "scale":
+        return [("grid",) + key[0][key[1]], ("spreadcopy", 0)]
+    if kind == "bias":
+        pair, c0, c1 = key
+        return [("scale", pair, n, c0, c1) for n in range(len(pair))] + [("spreadcopy", 1)]
     if kind == "grid":
         g, j, h = key
         return [("mix",) + key] + [("quant", "a", g, s) for s in range(PASSES["a"])] + [("quantl", "x", s, h) for s in range(LAID["x"])]
-    before = {"scale": "grid", "bias": "scale", "tanh": "bias", "colcopy": "cols", "spread": "colcopy", "spreadcopy": "spread"}
+    before = {"tanh": "bias", "colcopy": "cols", "spreadcopy": "spread"}
     if kind in ("spread",):
         return [("colcopy",)]
     return [(before[kind],) + key] if kind in before else []
@@ -48,7 +71,7 @@ def tile_weather_grid_channel_mixing_s2_kernel(tc, x, a, w, cell, chan, b, out):
     with ExitStack() as ctx:
         keep = ctx.enter_context(tc.tile_pool(name="keep", bufs=1))
         stage = ctx.enter_context(tc.tile_pool(name="stage", bufs=12))
-        epi = ctx.enter_context(tc.tile_pool(name="epi", bufs=4))
+        epi = ctx.enter_context(tc.tile_pool(name="epi", bufs=8))
         psum = ctx.enter_context(tc.psum_pool(name="psum", bufs=8))
         ctx.enter_context(tc.manual_schedule())
 
@@ -64,9 +87,6 @@ def tile_weather_grid_channel_mixing_s2_kernel(tc, x, a, w, cell, chan, b, out):
         for g in range(GROUPS):
             raw["x", g] = kept([P, J, CHANNELS], BF16, "x_raw%d" % g)
             raw["a", g] = kept([P, J, CELLS], BF16, "a_raw%d" % g)
-        for s in range(LAID["w"]):
-            for h in range(2):
-                raw["w", s, h] = kept([P, J, HALF], BF16, "w_raw%d%d" % (s, h))
         rows = kept([P, P], BF16, "rows")
         cells = kept([P, GROUPS, J], BF16, "cells")
         warm = kept([P, 1], F32, "warm")
@@ -89,14 +109,15 @@ def tile_weather_grid_channel_mixing_s2_kernel(tc, x, a, w, cell, chan, b, out):
 
         def load_w(h):
             for s in range(LAID["w"]):
+                raw["w", s, h] = kept([P, J, HALF], BF16, "w_raw%d%d" % (s, h))
                 nc.sync.dma_start(out=raw["w", s, h][:], in_=w_v[s][:, :, h * HALF : (h + 1) * HALF])
 
         load("x", 0)
         nc.sync.dma_start(out=rows[0:8, :], in_=chan.rearrange("(m n) -> m n", n=P))
         nc.sync.dma_start(out=rows[8:16, :], in_=b.rearrange("(m n) -> m n", n=P))
         load("x", 1)
-        load_w(0)
         load("x", 2)
+        load_w(0)
         load("a", 0)
         nc.sync.dma_start(out=cells[:], in_=cell.rearrange("(g p j) -> p g j", p=P, j=J))
         load("a", 1)
@@ -134,7 +155,17 @@ def tile_weather_grid_channel_mixing_s2_kernel(tc, x, a, w, cell, chan, b, out):
                     for u in range(2):
                         first = (2 * jp + jj) * (width // 2) + 256 * s
                         q = 2 * jj + u
-                        nc.tensor.transpose(tp[:, q * P : (q + 1) * P], words[:, first + u : first + 256 : 2], ident[:])
+                        if (k, g) in SORTED:
+                            src = tiles[("sort",) + key][:, q * P : (q + 1) * P]
+                        else:
+                            src = words[:, first + u : first + 256 : 2]
+                        nc.tensor.transpose(tp[:, q * P : (q + 1) * P], src, ident[:])
+            elif kind == "sort":
+                k, g, s, jp = key
+                tiles[op] = srt = stage.tile([P, 512], F32, name="srt", bufs=5, align_bytes=64)
+                js = slice(2 * jp, 2 * jp + 2)
+                words = raw[k, g][:].bitcast(F32)[:, js, 256 * s : 256 * (s + 1)]
+                copier(eng)(out=srt[:].rearrange("p (jj u i) -> p jj u i", jj=2, u=2), in_=words.rearrange("p jj (i u) -> p jj u i", u=2))
             elif kind == "copy":
                 k, g, s, jp = key
                 if ("grp", k, g, s) not in tiles:
@@ -172,25 +203,35 @@ def tile_weather_grid_channel_mixing_s2_kernel(tc, x, a, w, cell, chan, b, out):
                         stop=(kind == "grid" and s == PASSES[k] - 1),
                     )
             elif kind == "scale":
-                g, j, h = key
-                tiles[op] = z = epi.tile([P, HALF], F32, name="z")
+                pair, n, c0, c1 = key
+                if ("z", pair) not in tiles:
+                    tiles["z", pair] = epi.tile([P, len(pair), HALF], F32, name="z")
+                g, j, h = pair[n]
                 nc.vector.scalar_tensor_tensor(
-                    out=z[:], in0=tiles[("acc",) + key][:], scalar=cells[:, g, j : j + 1], in1=spread[0][:, h * HALF : (h + 1) * HALF], op0=ALU.mult, op1=ALU.mult
+                    out=tiles["z", pair][:, n, c0:c1],
+                    in0=tiles["acc", g, j, h][:, c0:c1],
+                    scalar=cells[:, g, j : j + 1],
+                    in1=spread[0][:, h * HALF + c0 : h * HALF + c1],
+                    op0=ALU.mult,
+                    op1=ALU.mult,
                 )
             elif kind == "bias":
-                g, j, h = key
-                tiles[op] = y = epi.tile([P, HALF], F32, name="y")
-                nc.vector.tensor_tensor(out=y[:], in0=tiles[("scale",) + key][:], in1=spread[1][:, h * HALF : (h + 1) * HALF], op=ALU.add)
+                pair, c0, c1 = key
+                h = pair[0][2]
+                b_cols = spread[1][:, h * HALF + c0 : h * HALF + c1].unsqueeze(1).to_broadcast([P, len(pair), c1 - c0])
+                z = tiles["z", pair][:, :, c0:c1]
+                nc.vector.tensor_tensor(out=z, in0=z, in1=b_cols, op=ALU.add)
             elif kind == "tanh":
-                g, j, h = key
-                o = epi.tile([P, HALF], F32, name="o")
-                nc.scalar.activation(out=o[:], in_=tiles[("bias",) + key][:], func=ACT.Tanh)
-                nc.sync.dma_start(out=out_v[g][:, j, h * HALF : (h + 1) * HALF], in_=o[:])
+                pair, c0, c1 = key
+                g, j, h = pair[0]
+                z = tiles["z", pair][:, :, c0:c1]
+                nc.scalar.activation(out=z, in_=z, func=ACT.Tanh)
+                nc.sync.dma_start(out=out_v[g][:, j : j + len(pair), h * HALF + c0 : h * HALF + c1], in_=z)
             elif kind == "cols":
                 tiles[op] = ps = bank("cols_ps", BF16)
                 nc.tensor.transpose(ps[:, 0:P], rows[:], ident_bf[:])
             elif kind == "colcopy":
-                nc.vector.tensor_copy(out=cols[:], in_=tiles[("cols",)][:, 0:16])
+                copier(eng)(out=cols[:], in_=tiles[("cols",)][:, 0:16])
             elif kind == "spread":
                 v = key[0]
                 tiles[op] = ps = bank("spread_ps", BF16)
@@ -199,41 +240,36 @@ def tile_weather_grid_channel_mixing_s2_kernel(tc, x, a, w, cell, chan, b, out):
             elif kind == "spreadcopy":
                 copier(eng)(out=spread[key[0]][:], in_=tiles[("spread",) + key][:])
 
-        def turns(kind, k, g):
-            return [(kind, k, g, s, jp) for jp in range(2) for s in range(PASSES[k])]
-
-        def quants(k, g):
-            return [("quant", k, g, s) for s in range(PASSES[k])]
-
         units = [(g, j, h) for h in range(2) for g in range(GROUPS) for j in range(J)]
-        first = units[:J]
-        tensor = turns("turn", "x", 0) + [("cols",), ("spread", 0), ("spread", 1)] + turns("turn", "x", 1) + turns("turn", "x", 2) + turns("turn", "a", 0)
-        tensor += [("mix",) + u for u in first]
-        tensor += turns("turn", "a", 1)
-        tensor += [("grid",) + u for u in first]
-        tensor += turns("turn", "a", 2)
-        for u in units[J:]:
-            tensor += [("mix",) + u, ("grid",) + u]
+        singles = 4
+        pairs = [tuple(units[n : n + 2]) for n in range(0, len(units) - singles, 2)] + [(u,) for u in units[len(units) - singles :]]
+        steps = {"X": [("cols",), ("spread", 0), ("spread", 1)], "cc": [("colcopy",)], "Z0": [("spreadcopy", 0)], "Z1": [("spreadcopy", 1)]}
+        for k in "xa":
+            for g in range(GROUPS):
+                for jp in range(2):
+                    for letter, kind in (("T", "turn"), ("C", "copy"), ("P", "sort")):
+                        steps["%s%s%d%d" % (letter, k, g, jp)] = [(kind, k, g, s, jp) for s in range(PASSES[k])]
+                for s in range(PASSES[k]):
+                    steps["Q%s%d%d" % (k, g, s)] = [("quant", k, g, s)]
+        for k in "xw":
+            for s in range(LAID[k]):
+                for h in range(2):
+                    steps["I%s%d%d" % (k, s, h)] = [("lay", k, s, h)]
+                    steps["L%s%d%d" % (k, s, h)] = [("quantl", k, s, h)]
+        for g, j, h in units:
+            steps["M%d%d%d" % (g, j, h)] = [("mix", g, j, h)]
+            steps["G%d%d%d" % (g, j, h)] = [("grid", g, j, h)]
+        for m, pair in enumerate(pairs):
+            parts = [(0, HALF)] if pair != pairs[-1] else [(0, HALF // 2), (HALF // 2, HALF)]
+            for i in range(len(pair)):
+                steps["S%d.%d" % (m, i)] = [("scale", pair, i) + c for c in parts]
+            steps["A%d" % m] = [("bias", pair) + c for c in parts]
+            steps["H%d" % m] = [("tanh", pair) + c for c in parts]
 
-        lay = lambda k, s, h: ("lay", k, s, h)
-        ql = lambda k, s, h: ("quantl", k, s, h)
-        scalar = turns("copy", "x", 0) + [("spreadcopy", 0), ("spreadcopy", 1)] + turns("copy", "x", 1) + [lay("w", 0, 0)] + turns("copy", "x", 2)[:2] + [lay("x", 2, 0)]
-        scalar += turns("copy", "a", 0) + turns("copy", "a", 1) + [lay("x", 1, 1)] + turns("copy", "a", 2)
-        vector = [lay("x", 0, 0), ("colcopy",), lay("x", 1, 0)] + quants("x", 0) + [lay("w", 1, 0), ql("x", 0, 0)] + quants("x", 1)
-        vector += [ql("w", 0, 0), ql("w", 1, 0)] + turns("copy", "x", 2)[2:] + [ql("x", 1, 0)] + quants("x", 2) + [ql("x", 2, 0)]
-        vector += quants("a", 0) + [lay("x", 0, 1)] + quants("a", 1) + [ql("x", 0, 1)]
-        v_after = {0: [lay("x", 2, 1)], 2: quants("a", 2)[:1], 3: quants("a", 2)[1:2], 4: quants("a", 2)[2:] + [ql("x", 1, 1)],
-                   5: [lay("w", 0, 1)], 6: [ql("x", 2, 1)], 7: [ql("w", 0, 1)], 8: [ql("w", 1, 1)]}
-        s_after = {0: [lay("w", 1, 1)]}
-        for n, u in enumerate(units):
-            vector.append(("scale",) + u)
-            if n:
-                vector.append(("bias",) + units[n - 1])
-            vector += v_after.get(n, [])
-            scalar.append(("tanh",) + u)
-            scalar += s_after.get(n, [])
-        vector.append(("bias",) + units[-1])
+        def listed(text):
+            return [op for step in text.split() for op in steps[step]]
 
+        tensor, vector, scalar = listed(TENSOR), listed(VECTOR), listed(SCALAR)
         queues = {"tensor": tensor, "vector": vector, "scalar": scalar}
         done = set()
         while any(queues.values()):

@@ -22,18 +22,18 @@ GROUPS = CELLS // 512
 PASSES = {"x": CHANNELS // 512, "a": CELLS // 512}
 SORTED = [("a", 1), ("a", 2)]
 TENSOR = """
-Tx00 Tx01 X Tx11 Tx10 Tx20 Tx21 Ta00 Ta01 M000 M010 Ta10 M020 Ta11 G000 G010 G020 M030 Ta21 M100 M110 G030 G100 M120
-G110 M130 G120 Ta20 M200 M210 G130 M220 M230 G200 G210 G220 M001 G230 M011 M021 M031 M101 G001 G011 G021 G031 G101 M111
-G111 M121 G121 M131 G131 M201 G201 M211 G211 M221 G221 M231 G231
+Tx00 Tx01 X Tx10 Tx11 Tx20 Tx21 M000 Ta00 Ta01 M010 M020 Ta10 M030 M100 Ta11 G000 G010 G020 M110 G030 Ta21 G100 Ta20
+G110 M120 M130 G120 G130 M200 M210 G200 M220 G210 G220 M230 G230 M001 M011 M021 G001 G011 G021 M031 M101 M111 G031 G101
+G111 M121 G121 M131 M201 G131 G201 M211 M221 G211 G221 M231 G231
 """
 VECTOR = """
-Ix01 Ix00 Qx01 Qx00 Lx01 Ix20 Cx10 Iw10 Qx10 Lw10 Lx00 Lw00 Lx10 Lx20 Pa10 Qa00 Pa11 Qa02 Qa01 Qx21 Qx11 Qx20 Qa10 S0.0
-Qa12 S0.1 Qa11 S1.0 A0 Pa20 S1.1 S2.0 A1 S2.1 Lw11 A2 S3.0 Qa20 Qa21 Qa22 S3.1 Lw01 Lx11 A3 S4.0 S4.1 S5.0 Lx21 S5.1 A4
-A5 S6.0 S6.1 S7.0 S7.1 A6 S8.0 A7 S8.1 S9.0 A8 S9.1 S10.0 A9 A10 S11.0 S12.0 A11 A12 S13.0 A13
+Ix01 cc Ix00 Iw10 Qx01 Qx00 Lw00 Lw10 Ix10 Lx01 Ix20 Lx00 Lx11 Lx20 Qx10 Qx11 Lx10 Pa10 Qa01 Qa02 Pa11 Qa00 Qx20 Qx21
+Qa10 S0.0 Qa11 S0.1 Qa12 S1.0 S1.1 A0 A1 S2.0 Qa20 Qa21 S2.1 Qa22 A2 S3.0 S3.1 Lw01 S4.0 A3 Lw11 S4.1 Lx21 S5.0 S5.1 A4
+S6.0 S6.1 S7.0 A5 A6 S7.1 S8.0 S8.1 A7 A8 S9.0 S9.1 S10.0 A9 A10 S11.0 S12.0 A11 A12 S13.0 A13
 """
 SCALAR = """
-Cx00 Cx01 cc Ix10 Z0 Cx11 Iw00 Cx20 Ca00 Ca01 Cx21 Ca10 Ca11 Pa21 Z1 Iw01 Iw11 Ca21 Ca20 Ix11 Ix21 H0 H1 H2 H3 H4 H5 H6
-H7 H8 H9 H10 H11 H12 H13
+Cx00 Cx01 Iw00 Z0 Cx10 Ix11 Cx11 Cx20 Z1 Ca00 Ca01 Cx21 Ca10 Ca11 Pa21 Pa20 Ca21 Ca20 Iw01 Iw11 Ix21 H0 H1 H2 H3 H4 H5
+H6 H7 H8 H9 H10 H11 H12 H13
 """
 LAID = {"w": CHANNELS // 512, "x": CELLS // 512}
 
@@ -115,9 +115,9 @@ def tile_weather_grid_channel_mixing_s2_kernel(tc, x, a, w, cell, chan, b, out):
         load("x", 0)
         nc.sync.dma_start(out=rows[0:8, :], in_=chan.rearrange("(m n) -> m n", n=P))
         nc.sync.dma_start(out=rows[8:16, :], in_=b.rearrange("(m n) -> m n", n=P))
+        load_w(0)
         load("x", 1)
         load("x", 2)
-        load_w(0)
         load("a", 0)
         nc.sync.dma_start(out=cells[:], in_=cell.rearrange("(g p j) -> p g j", p=P, j=J))
         load("a", 1)

from contextlib import ExitStack

import concourse.mybir as mybir
from concourse.masks import make_identity

CELLS, CHANNELS = 1536, 1024
FLOPS = 2 * CELLS * CELLS * CHANNELS + 2 * CELLS * CHANNELS * CHANNELS

F32 = mybir.dt.float32
BF16 = mybir.dt.bfloat16
U32 = mybir.dt.uint32
U8 = mybir.dt.uint8
E4M3 = mybir.dt.float8_e4m3fn_x4
E5M2 = mybir.dt.float8_e5m2_x4
ALU = mybir.AluOpType
ACT = mybir.ActivationFunctionType

P = 128
J = 4
HALF = 512
GROUPS = CELLS // 512
PASSES = {"x": CHANNELS // 512, "a": CELLS // 512}
SORTED = [("a", 1), ("a", 2)]
TENSOR = """
Tx00 Tx01 X Tx10 Tx11 Tx20 Tx21 M000 Ta00 Ta01 M010 M020 Ta10 M030 M100 Ta11 G000 G010 G020 M110 G030 Ta21 G100 Ta20
G110 M120 M130 G120 G130 M200 M210 G200 M220 G210 G220 M230 G230 M001 M011 M021 G001 G011 G021 M031 M101 M111 G031 G101
G111 M121 G121 M131 M201 G131 G201 M211 M221 G211 G221 M231 G231
"""
VECTOR = """
Ix01 cc Ix00 Iw10 Qx01 Qx00 Lw00 Lw10 Ix10 Lx01 Ix20 Lx00 Lx11 Lx20 Qx10 Qx11 Lx10 Pa10 Qa01 Qa02 Pa11 Qa00 Qx20 Qx21
Qa10 S0.0 Qa11 S0.1 Qa12 S1.0 S1.1 A0 A1 S2.0 Qa20 Qa21 S2.1 Qa22 A2 S3.0 S3.1 Lw01 S4.0 A3 Lw11 S4.1 Lx21 S5.0 S5.1 A4
S6.0 S6.1 S7.0 A5 A6 S7.1 S8.0 S8.1 A7 A8 S9.0 S9.1 S10.0 A9 A10 S11.0 S12.0 A11 A12 S13.0 A13
"""
SCALAR = """
Cx00 Cx01 Iw00 Z0 Cx10 Ix11 Cx11 Cx20 Z1 Ca00 Ca01 Cx21 Ca10 Ca11 Pa21 Pa20 Ca21 Ca20 Iw01 Iw11 Ix21 H0 H1 H2 H3 H4 H5
H6 H7 H8 H9 H10 H11 H12 H13
"""
LAID = {"w": CHANNELS // 512, "x": CELLS // 512}


def producers(op):
    kind, key = op[0], op[1:]
    if kind == "turn":
        k, g, s, jp = key
        return [("sort",) + key] if (k, g) in SORTED else []
    if kind == "copy":
        return [("turn",) + key]
    if kind == "quant":
        return [("copy",) + key + (jp,) for jp in range(2)]
    if kind == "quantl":
        return [("lay",) + key]
    if kind == "mix":
        g, j, h = key
        return [("quant", "x", g, s) for s in range(PASSES["x"])] + [("quantl", "w", s, h) for s in range(LAID["w"])]
    if kind == "scale":
        return [("grid",) + key[0][key[1]], ("spreadcopy", 0)]
    if kind == "bias":
        pair, c0, c1 = key
        return [("scale", pair, n, c0, c1) for n in range(len(pair))] + [("spreadcopy", 1)]
    if kind == "grid":
        g, j, h = key
        return [("mix",) + key] + [("quant", "a", g, s) for s in range(PASSES["a"])] + [("quantl", "x", s, h) for s in range(LAID["x"])]
    before = {"tanh": "bias", "colcopy": "cols", "spreadcopy": "spread"}
    if kind in ("spread",):
        return [("colcopy",)]
    return [(before[kind],) + key] if kind in before else []


def tile_weather_grid_channel_mixing_s2_kernel(tc, x, a, w, cell, chan, b, out):
    nc = tc.nc
    with ExitStack() as ctx:
        keep = ctx.enter_context(tc.tile_pool(name="keep", bufs=1))
        stage = ctx.enter_context(tc.tile_pool(name="stage", bufs=12))
        epi = ctx.enter_context(tc.tile_pool(name="epi", bufs=8))
        psum = ctx.enter_context(tc.psum_pool(name="psum", bufs=8))
        ctx.enter_context(tc.manual_schedule())

        def kept(shape, dtype, name):
            return keep.tile(shape, dtype, name=name, align_bytes=64)

        x_v = x.rearrange("(g p j) c -> g p j c", p=P, j=J)
        a_v = a.rearrange("(g p j) c -> g p j c", p=P, j=J)
        w_v = w.rearrange("(s p j) c -> s p j c", p=P, j=J)
        out_v = out.rearrange("(g p j) c -> g p j c", p=P, j=J)

        raw = {}
        for g in range(GROUPS):
            raw["x", g] = kept([P, J, CHANNELS], BF16, "x_raw%d" % g)
            raw["a", g] = kept([P, J, CELLS], BF16, "a_raw%d" % g)
        rows = kept([P, P], BF16, "rows")
        cells = kept([P, GROUPS, J], BF16, "cells")
        warm = kept([P, 1], F32, "warm")
        ident = kept([P, P], F32, "ident")
        ident_bf = kept([P, P], BF16, "ident_bf")
        cols = kept([P, 16], BF16, "cols")
        spread = [kept([P, CHANNELS], BF16, "spread%d" % v) for v in range(2)]

        nc.vector.memset(warm[:], 0.0)
        nc.scalar.activation(out=warm[:], in_=warm[:], func=ACT.Tanh)
        nc.vector.memset(rows[:], 0.0)
        make_identity(nc, ident[:])
        nc.vector.tensor_copy(out=ident_bf[:], in_=ident[:])

        def load(k, g):
            view = {"x": x_v, "a": a_v}[k]
            for jp in range(2):
                js = slice(2 * jp, 2 * jp + 2)
                nc.sync.dma_start(out=raw[k, g][:, js, :], in_=view[g][:, js, :])

        def load_w(h):
            for s in range(LAID["w"]):
                raw["w", s, h] = kept([P, J, HALF], BF16, "w_raw%d%d" % (s, h))
                nc.sync.dma_start(out=raw["w", s, h][:], in_=w_v[s][:, :, h * HALF : (h + 1) * HALF])

        load("x", 0)
        nc.sync.dma_start(out=rows[0:8, :], in_=chan.rearrange("(m n) -> m n", n=P))
        nc.sync.dma_start(out=rows[8:16, :], in_=b.rearrange("(m n) -> m n", n=P))
        load_w(0)
        load("x", 1)
        load("x", 2)
        load("a", 0)
        nc.sync.dma_start(out=cells[:], in_=cell.rearrange("(g p j) -> p g j", p=P, j=J))
        load("a", 1)
        load("a", 2)
        load_w(1)

        codes, scales = {}, {}
        for k in "xa":
            for g in range(GROUPS):
                for s in range(PASSES[k]):
                    codes[k, "t", g, s] = kept([P, HALF], U32, "c%st%d%d" % (k, g, s))
                    scales[k, "t", g, s] = kept([P, HALF], U8, "s%st%d%d" % (k, g, s))
        for k in "xw":
            for s in range(LAID[k]):
                for h in range(2):
                    codes[k, "l", s, h] = kept([P, HALF], U32, "c%sl%d%d" % (k, s, h))
                    scales[k, "l", s, h] = kept([P, HALF], U8, "s%sl%d%d" % (k, s, h))

        tiles = {}

        def bank(name, dtype=F32):
            return psum.tile([P, 512 if dtype == F32 else 1024], dtype, name=name, tag="bank")

        def copier(eng):
            return nc.vector.tensor_copy if eng == "vector" else nc.scalar.copy

        def emit(eng, op):
            kind, key = op[0], op[1:]
            if kind == "turn":
                k, g, s, jp = key
                width = {"x": CHANNELS, "a": CELLS}[k]
                words = raw[k, g][:].rearrange("p j k -> p (j k)").bitcast(F32)
                tiles[op] = tp = bank("tp")
                for jj in range(2):
                    for u in range(2):
                        first = (2 * jp + jj) * (width // 2) + 256 * s
                        q = 2 * jj + u
                        if (k, g) in SORTED:
                            src = tiles[("sort",) + key][:, q * P : (q + 1) * P]
                        else:
                            src = words[:, first + u : first + 256 : 2]
                        nc.tensor.transpose(tp[:, q * P : (q + 1) * P], src, ident[:])
            elif kind == "sort":
                k, g, s, jp = key
                tiles[op] = srt = stage.tile([P, 512], F32, name="srt", bufs=5, align_bytes=64)
                js = slice(2 * jp, 2 * jp + 2)
                words = raw[k, g][:].bitcast(F32)[:, js, 256 * s : 256 * (s + 1)]
                copier(eng)(out=srt[:].rearrange("p (jj u i) -> p jj u i", jj=2, u=2), in_=words.rearrange("p jj (i u) -> p jj u i", u=2))
            elif kind == "copy":
                k, g, s, jp = key
                if ("grp", k, g, s) not in tiles:
                    tiles["grp", k, g, s] = stage.tile([P, J * HALF], BF16, name="grp", align_bytes=64)
                grp = tiles["grp", k, g, s]
                o = grp[:].bitcast(F32)[:, jp * 512 : (jp + 1) * 512].rearrange("p (jj m u) -> p jj m u", jj=2, u=2)
                i = tiles[("turn",) + key][:].rearrange("p (jj u m) -> p jj m u", jj=2, u=2)
                copier(eng)(out=o, in_=i)
            elif kind == "quant":
                k, g, s = key
                fmt = E5M2 if k == "x" else E4M3
                nc.vector.quantize_mx(out=codes[k, "t", g, s][:].bitcast(fmt), scales=scales[k, "t", g, s][:], in_=tiles["grp", k, g, s][:])
            elif kind == "lay":
                k, s, h = key
                tiles[op] = grp = stage.tile([P, J * HALF], BF16, name="grp", align_bytes=64)
                src = raw["w", s, h][:] if k == "w" else raw["x", s][:, :, h * HALF : (h + 1) * HALF]
                copier(eng)(out=grp[:].rearrange("p (c i j) -> p c j i", i=4, j=J), in_=src.rearrange("p j (c i) -> p c j i", i=4))
            elif kind == "quantl":
                k, s, h = key
                nc.vector.quantize_mx(out=codes[k, "l", s, h][:].bitcast(E4M3), scales=scales[k, "l", s, h][:], in_=tiles["lay", k, s, h][:])
            elif kind in ("mix", "grid"):
                g, j, h = key
                if kind == "mix":
                    tiles[("acc",) + key] = bank("acc")
                k, r, fmt = ("x", "w", E5M2) if kind == "mix" else ("a", "x", E4M3)
                js = slice(j * P, (j + 1) * P)
                for s in range(PASSES[k]):
                    nc.tensor.matmul_mx(
                        out=tiles[("acc",) + key][:],
                        lhsT=codes[k, "t", g, s][:, js].bitcast(fmt),
                        lhsT_scale=scales[k, "t", g, s][:, js],
                        rhs=codes[r, "l", s, h][:].bitcast(E4M3),
                        rhs_scale=scales[r, "l", s, h][:],
                        start=(kind == "mix" and s == 0),
                        stop=(kind == "grid" and s == PASSES[k] - 1),
                    )
            elif kind == "scale":
                pair, n, c0, c1 = key
                if ("z", pair) not in tiles:
                    tiles["z", pair] = epi.tile([P, len(pair), HALF], F32, name="z")
                g, j, h = pair[n]
                nc.vector.scalar_tensor_tensor(
                    out=tiles["z", pair][:, n, c0:c1],
                    in0=tiles["acc", g, j, h][:, c0:c1],
                    scalar=cells[:, g, j : j + 1],
                    in1=spread[0][:, h * HALF + c0 : h * HALF + c1],
                    op0=ALU.mult,
                    op1=ALU.mult,
                )
            elif kind == "bias":
                pair, c0, c1 = key
                h = pair[0][2]
                b_cols = spread[1][:, h * HALF + c0 : h * HALF + c1].unsqueeze(1).to_broadcast([P, len(pair), c1 - c0])
                z = tiles["z", pair][:, :, c0:c1]
                nc.vector.tensor_tensor(out=z, in0=z, in1=b_cols, op=ALU.add)
            elif kind == "tanh":
                pair, c0, c1 = key
                g, j, h = pair[0]
                z = tiles["z", pair][:, :, c0:c1]
                nc.scalar.activation(out=z, in_=z, func=ACT.Tanh)
                nc.sync.dma_start(out=out_v[g][:, j : j + len(pair), h * HALF + c0 : h * HALF + c1], in_=z)
            elif kind == "cols":
                tiles[op] = ps = bank("cols_ps", BF16)
                nc.tensor.transpose(ps[:, 0:P], rows[:], ident_bf[:])
            elif kind == "colcopy":
                copier(eng)(out=cols[:], in_=tiles[("cols",)][:, 0:16])
            elif kind == "spread":
                v = key[0]
                tiles[op] = ps = bank("spread_ps", BF16)
                for m in range(8):
                    nc.tensor.transpose(ps[:, m * P : (m + 1) * P], cols[:, 8 * v + m : 8 * v + m + 1].to_broadcast([P, P]), ident_bf[:])
            elif kind == "spreadcopy":
                copier(eng)(out=spread[key[0]][:], in_=tiles[("spread",) + key][:])

        units = [(g, j, h) for h in range(2) for g in range(GROUPS) for j in range(J)]
        singles = 4
        pairs = [tuple(units[n : n + 2]) for n in range(0, len(units) - singles, 2)] + [(u,) for u in units[len(units) - singles :]]
        steps = {"X": [("cols",), ("spread", 0), ("spread", 1)], "cc": [("colcopy",)], "Z0": [("spreadcopy", 0)], "Z1": [("spreadcopy", 1)]}
        for k in "xa":
            for g in range(GROUPS):
                for jp in range(2):
                    for letter, kind in (("T", "turn"), ("C", "copy"), ("P", "sort")):
                        steps["%s%s%d%d" % (letter, k, g, jp)] = [(kind, k, g, s, jp) for s in range(PASSES[k])]
                for s in range(PASSES[k]):
                    steps["Q%s%d%d" % (k, g, s)] = [("quant", k, g, s)]
        for k in "xw":
            for s in range(LAID[k]):
                for h in range(2):
                    steps["I%s%d%d" % (k, s, h)] = [("lay", k, s, h)]
                    steps["L%s%d%d" % (k, s, h)] = [("quantl", k, s, h)]
        for g, j, h in units:
            steps["M%d%d%d" % (g, j, h)] = [("mix", g, j, h)]
            steps["G%d%d%d" % (g, j, h)] = [("grid", g, j, h)]
        for m, pair in enumerate(pairs):
            parts = [(0, HALF)] if pair != pairs[-1] else [(0, HALF // 2), (HALF // 2, HALF)]
            for i in range(len(pair)):
                steps["S%d.%d" % (m, i)] = [("scale", pair, i) + c for c in parts]
            steps["A%d" % m] = [("bias", pair) + c for c in parts]
            steps["H%d" % m] = [("tanh", pair) + c for c in parts]

        def listed(text):
            return [op for step in text.split() for op in steps[step]]

        tensor, vector, scalar = listed(TENSOR), listed(VECTOR), listed(SCALAR)
        queues = {"tensor": tensor, "vector": vector, "scalar": scalar}
        done = set()
        while any(queues.values()):
            for eng, queue in queues.items():
                if queue and all(d in done for d in producers(queue[0])):
                    op = queue.pop(0)
                    emit(eng, op)
                    done.add(op)
